import numpy as np
import ml_dtypes


def mxq(x, axis, fmt="e4m3"):
    dtype, down = {"e4m3": (ml_dtypes.float8_e4m3fn, 7), "e5m2": (ml_dtypes.float8_e5m2, 14)}[fmt]
    v = np.moveaxis(np.asarray(x, np.float32).astype(ml_dtypes.bfloat16).astype(np.float64), axis, -1)
    blocks = v.reshape(v.shape[:-1] + (-1, 32))
    amax = np.abs(blocks).max(-1, keepdims=True)
    byte = np.maximum(np.where(amax > 0, np.frexp(amax)[1] - 1 + 127, 0) - down, 1)
    scale = np.exp2(byte - 127.0)
    codes = (blocks / scale).astype(np.float32).astype(dtype).astype(np.float64)
    return np.moveaxis((codes * scale).reshape(v.shape), -1, axis)


WIDE = False


def mx_kscale(k):
    if not WIDE:
        return np.ones(k)
    levels = np.array([10, -10, 5, -5, 0])
    if k % 512:
        return np.exp2(np.random.permutation(np.resize(levels, k // 32))).repeat(32)
    a = np.empty((k // 512, 16))
    for p in range(k // 512):
        a[p, :8] = np.random.permutation(np.resize(levels, 8))
        for g in range(8):
            far = levels[np.abs(levels - a[p, g]) >= 10]
            a[p, g + 8] = far[np.random.randint(len(far))]
    return np.exp2(a.ravel()).repeat(32)


BF16 = ml_dtypes.bfloat16


def bf(x):
    return np.asarray(x, np.float32).astype(BF16)


def f64(x):
    return np.asarray(x).astype(np.float64)


S, F, G, T, C = 512, 512, 128, 128, 6144


def smooth_modulus(re, im):
    return np.sqrt(re * re + im * im + 0.25)


def draw0():
    s, t = mx_kscale(S), mx_kscale(F)
    a_scale = 1.0 / np.sqrt(S)
    c_scale = 1.5 / np.sqrt(F)
    return {
        "x": bf(np.random.standard_normal((S, C)) * s[:, None]),
        "ar": bf(np.random.standard_normal((F, S)) * a_scale / s[None, :]),
        "aim": bf(np.random.standard_normal((F, S)) * a_scale / s[None, :]),
        "g1": bf((1.0 + 0.1 * np.random.standard_normal(F)) * t),
        "cr": bf(np.random.standard_normal((G, F)) * c_scale / t[None, :]),
        "cim": bf(np.random.standard_normal((G, F)) * c_scale / t[None, :]),
        "phi": bf(np.random.standard_normal((T, F)) * c_scale / t[None, :]),
    }


def core(x, ar, aim, g1, cr, cim, phi):
    xq = mxq(f64(x), 0, "e4m3")
    r1 = mxq(f64(ar), 1, "e4m3") @ xq
    i1 = mxq(f64(aim), 1, "e4m3") @ xq
    u1 = smooth_modulus(r1, i1)
    n1 = f64(g1)[:, None] * (u1 - np.mean(u1, axis=0, keepdims=True))
    nq = mxq(n1, 0, "e4m3")
    s1 = mxq(f64(phi), 1, "e4m3") @ nq
    r2 = mxq(f64(cr), 1, "e4m3") @ nq
    i2 = mxq(f64(cim), 1, "e4m3") @ nq
    u2 = smooth_modulus(r2, i2)
    return s1, u2


def e4m3fn_bytes(y):
    return np.clip(np.asarray(y, np.float64), -448.0, 448.0).astype(np.float32).astype(ml_dtypes.float8_e4m3fn).view(np.uint8)


def e4m3fn_values(b):
    return np.asarray(b, np.uint8).view(ml_dtypes.float8_e4m3fn).astype(np.float64)


def setup_inputs():
    d = draw0()
    x0 = np.asarray(d['x']).astype(np.float64)
    s = (np.max(np.abs(x0), axis=(1,), keepdims=True) / 448.0).astype(np.float32)
    out = {}
    for k, v in d.items():
        if k == 'x':
            out['x_bytes'] = e4m3fn_bytes(x0 / s.astype(np.float64))
            out['x_scale'] = s
        else:
            out[k] = v
    return out


def reference(x_bytes, x_scale, ar, aim, g1, cr, cim, phi):
    return core(e4m3fn_values(x_bytes) * x_scale.astype(np.float64), ar, aim, g1, cr, cim, phi)

@@ -1,0 +1,416 @@
+from contextlib import ExitStack
+
+import concourse.mybir as mybir
+from concourse.masks import make_identity
+
+S, F, G, T, C = 512, 512, 128, 128, 6144
+
+F32 = mybir.dt.float32
+BF16 = mybir.dt.bfloat16
+U32 = mybir.dt.uint32
+U8 = mybir.dt.uint8
+FP8 = mybir.dt.float8_e4m3fn
+FP8X4 = mybir.dt.float8_e4m3fn_x4
+ACT = mybir.ActivationFunctionType
+ALU = mybir.AluOpType
+
+FLOPS = 2 * C * (2 * F * S + 2 * G * F + T * F)
+
+P = 128
+PAIR = 256
+N_PAIRS = C // PAIR
+N_FT = F // P
+CHUNKS = [256, 256] + [512] * 11
+LOADS = [256, 256, 512, 1024, 1024, 1024, 1024, 1024]
+
+
+def tile_learnedsecondorderscattering_t_kernel(
+    tc, x_bytes, x_scale, ar, aim, g1, cr, cim, phi, out_0, out_1
+):
+    nc = tc.nc
+    with ExitStack() as ctx:
+        keep = ctx.enter_context(tc.tile_pool(name="keep", bufs=1))
+        stage = ctx.enter_context(tc.tile_pool(name="stage", bufs=2))
+        psum = ctx.enter_context(tc.psum_pool(name="psum", bufs=1))
+        ident = keep.tile([P, P], F32, name="ident")
+        make_identity(nc, ident[:])
+        ctx.enter_context(tc.manual_schedule())
+
+        scale = keep.tile([P, 4], F32, name="scale")
+        nc.sync.dma_start(out=scale[:], in_=x_scale.rearrange("(p t) o -> p (t o)", t=4))
+        x_rows = x_bytes.rearrange("(p t) c -> p t c", t=4)
+        x_at = []
+
+        def load_x(i):
+            first = sum(LOADS[:i])
+            xb = keep.tile([P, 4, LOADS[i]], U8, name=f"xb{i}", align_bytes=64)
+            nc.sync.dma_start(out=xb[:], in_=x_rows[:, :, first : first + LOADS[i]])
+            x_at.append((first, first + LOADS[i], xb))
+
+        load_x(0)
+        quarter = keep.tile([P, 1], F32, name="quarter")
+        nc.vector.memset(quarter[:], 0.25)
+        warm = keep.tile([P, 1], F32, name="warm")
+        nc.scalar.activation(out=warm[:], in_=quarter[:], func=ACT.Sqrt)
+
+        bank_rows = {}
+        for u in range(2):
+            for name, w in (("ar", ar), ("aim", aim)):
+                rows = keep.tile([P, 2, S], BF16, name=f"{name}_rows{u}", align_bytes=64)
+                nc.sync.dma_start(
+                    out=rows[:], in_=w.rearrange("(q s) k -> q s k", s=4)[:, 2 * u : 2 * u + 2, :]
+                )
+                bank_rows[name, u] = rows
+        load_x(1)
+        w2_rows = keep.tile([P, 3, F], BF16, name="w2_rows", align_bytes=64)
+        for m, w in enumerate((cr, cim, phi)):
+            nc.sync.dma_start(out=w2_rows[:, m, :], in_=w)
+        load_x(2)
+        g_plain = keep.tile([P, F], BF16, name="g_plain")
+        nc.sync.dma_start(out=g_plain[:], in_=g1.partition_broadcast(P))
+        for i in range(3, len(LOADS)):
+            load_x(i)
+
+        x_wide, x_grouped, x_codes, x_planes = {}, {}, {}, {}
+
+        def chunk_first(k):
+            return sum(CHUNKS[:k])
+
+        def widen(k):
+            n = CHUNKS[k]
+            first = chunk_first(k)
+            wide = stage.tile([P, 4, n], BF16, name="x_wide", align_bytes=64)
+            for lo, hi, xb in x_at:
+                if lo <= first < hi:
+                    for t in range(4):
+                        nc.vector.tensor_scalar(
+                            out=wide[:, t, :],
+                            in0=xb[:, t, first - lo : first - lo + n].bitcast(FP8),
+                            scalar1=scale[:, t : t + 1],
+                            scalar2=None,
+                            op0=ALU.mult,
+                        )
+            x_wide[k] = wide
+
+        def group(k, half):
+            n = CHUNKS[k]
+            if half == 0:
+                grouped = stage.tile([P, n, 4], BF16, name="x_grouped", align_bytes=64)
+                x_grouped[k] = grouped
+            cols = slice(half * n // 2, (half + 1) * n // 2)
+            nc.vector.tensor_copy(
+                out=x_grouped[k][:, cols, :], in_=x_wide[k][:, :, cols].rearrange("p t c -> p c t")
+            )
+
+        def quantize_x(k):
+            n = CHUNKS[k]
+            codes = stage.tile([P, n], U32, name="x_codes", bufs=3, align_bytes=64)
+            planes = stage.tile([P, n], U8, name="x_planes", bufs=3, align_bytes=64)
+            nc.vector.quantize_mx(
+                out=codes[:].bitcast(FP8X4),
+                scales=planes[:],
+                in_=x_grouped[k][:].rearrange("p c t -> p (c t)"),
+            )
+            x_codes[k], x_planes[k] = codes, planes
+
+        a_grouped = {n: keep.tile([P, F, 4], BF16, name=f"{n}_grouped", align_bytes=64) for n in ("ar", "aim")}
+        a_codes = {n: keep.tile([P, F], U32, name=f"{n}_codes", align_bytes=64) for n in ("ar", "aim")}
+        a_planes = {n: keep.tile([P, F], U8, name=f"{n}_planes", align_bytes=64) for n in ("ar", "aim")}
+
+        def turn_a(name, u):
+            turned = psum.tile([P, 2, 2, P], F32, name="turned", tag="sq", bufs=4)
+            for e in range(2):
+                words = bank_rows[name, u][:, e, :].bitcast(F32)
+                for v in range(2):
+                    nc.tensor.transpose(turned[:, e, v, :], words[:, v : S // 2 : 2], ident[:])
+            return turned
+
+        def group_a(name, u, turned):
+            nc.scalar.copy(
+                out=a_grouped[name][:, u * 256 : u * 256 + 256, :].bitcast(F32).rearrange("p (q e) v -> p q e v", e=2),
+                in_=turned[:].rearrange("p e v q -> p q e v"),
+            )
+
+        def quantize_a(name, u):
+            cols = slice(u * 256, u * 256 + 256)
+            nc.vector.quantize_mx(
+                out=a_codes[name][:, cols].bitcast(FP8X4),
+                scales=a_planes[name][:, cols],
+                in_=a_grouped[name][:, cols, :].rearrange("p j t -> p (j t)"),
+            )
+
+        w2_grouped = keep.tile([P, 3, P, 4], BF16, name="w2_grouped", align_bytes=64)
+        w2_codes = keep.tile([P, 3 * P], U32, name="w2_codes", align_bytes=64)
+        w2_planes = keep.tile([P, 3 * P], U8, name="w2_planes", align_bytes=64)
+        w2_turned = []
+
+        def turn_w2():
+            for ms in ((0, 1), (2,)):
+                turned = psum.tile([P, 2, 2, P], F32, name="turned2", tag="c", bufs=2)
+                for i, m in enumerate(ms):
+                    words = w2_rows[:, m, :].bitcast(F32)
+                    for v in range(2):
+                        nc.tensor.transpose(turned[:, i, v, :], words[:, v : F // 2 : 2], ident[:])
+                w2_turned.append((ms, turned))
+
+        def group_w2():
+            for ms, turned in w2_turned:
+                nc.vector.tensor_copy(
+                    out=w2_grouped[:, ms[0] : ms[-1] + 1, :, :].bitcast(F32),
+                    in_=turned[:, 0 : len(ms), :, :].rearrange("p m v g -> p m g v"),
+                )
+
+        def quantize_w2():
+            for lo, hi in ((0, 2), (2, 3)):
+                nc.vector.quantize_mx(
+                    out=w2_codes[:, lo * P : hi * P].bitcast(FP8X4),
+                    scales=w2_planes[:, lo * P : hi * P],
+                    in_=w2_grouped[:, lo:hi, :, :].rearrange("p m g t -> p (m g t)"),
+                )
+
+        sq_banks, squares, c_banks, gains = {}, {}, {}, []
+        u1s, means, n1s, t_banks, n_grouped, n_codes, n_planes = {}, {}, {}, {}, {}, {}, {}
+        ri2_banks, o_banks, squares2 = {}, {}, {}
+
+        def where(p):
+            c = p * PAIR
+            for k in range(len(CHUNKS)):
+                first = chunk_first(k)
+                if first <= c < first + CHUNKS[k]:
+                    return k, slice(c - first, c - first + PAIR)
+            raise AssertionError("no chunk")
+
+        def first_bank(p, ft):
+            k, cols = where(p)
+            bank = psum.tile([P, 2, PAIR], F32, name="sq_bank", tag="sq", bufs=4)
+            rows = slice(ft * P, ft * P + P)
+            for i, n in enumerate(("ar", "aim")):
+                nc.tensor.matmul_mx(
+                    out=bank[:, i, :],
+                    lhsT=a_codes[n][:, rows].bitcast(FP8X4),
+                    lhsT_scale=a_planes[n][:, rows],
+                    rhs=x_codes[k][:, cols].bitcast(FP8X4),
+                    rhs_scale=x_planes[k][:, cols],
+                    start=True,
+                    stop=True,
+                )
+            sq_banks[p, ft] = bank
+
+        def square(p, ft):
+            sq = stage.tile([P, 2, PAIR], F32, name="square", bufs=10)
+            nc.scalar.activation(out=sq[:], in_=sq_banks[p, ft][:], func=ACT.Square)
+            squares[p, ft] = sq
+
+        def open_c(p):
+            c_banks[p] = []
+            for b in range(2):
+                bank = psum.tile([P, F], F32, name="c_bank", tag="c", bufs=2)
+                c_banks[p].append(bank)
+
+        def add_turned(p, b, fts):
+            for ft in fts:
+                for i in range(2):
+                    nc.tensor.matmul(
+                        out=c_banks[p][b][:, ft * P : ft * P + P],
+                        lhsT=squares[p, ft][:, i, b * P : b * P + P],
+                        rhs=ident[:],
+                        is_transpose=True,
+                        start=(i == 0),
+                        stop=(i == 1),
+                    )
+
+        def modulus(p):
+            for b in range(2):
+                total = stage.tile([P, 1], F32, name="total", bufs=6)
+                mean = stage.tile([P, 1], F32, name="mean", bufs=6)
+                u1 = stage.tile([P, F], F32, name="u1", bufs=4)
+                nc.scalar.activation(
+                    out=u1[:], in_=c_banks[p][b][:], func=ACT.Sqrt, bias=quarter[:, 0:1], accum_out=total[:, 0:1]
+                )
+                nc.gpsimd.tensor_scalar(out=mean[:], in0=total[:], scalar1=1.0 / F, scalar2=None, op0=ALU.mult)
+                u1s[p, b], means[p, b] = u1, mean
+
+        def centre(p):
+            n1s[p] = []
+            for b in range(2):
+                n1 = stage.tile([P, F], BF16, name="n1", bufs=4, align_bytes=64)
+                nc.vector.scalar_tensor_tensor(
+                    out=n1[:],
+                    in0=u1s[p, b][:],
+                    scalar=means[p, b][:, 0:1],
+                    in1=gains[0][:],
+                    op0=ALU.subtract,
+                    op1=ALU.mult,
+                )
+                n1s[p].append(n1)
+
+        def turn_n(p):
+            bank = psum.tile([P, 2, 2, P], F32, name="t_bank", tag="tr", bufs=1)
+            for b in range(2):
+                words = n1s[p][b][:].bitcast(F32)
+                for u in range(2):
+                    nc.tensor.transpose(bank[:, b, u, :], words[:, u * P : u * P + P], ident[:])
+            t_banks[p] = bank
+
+        def group_n(p):
+            grouped = stage.tile([P, PAIR, 4], BF16, name="n_grouped", bufs=2, align_bytes=64)
+            nc.vector.tensor_copy(
+                out=grouped[:].bitcast(F32).rearrange("p (b r) u -> p b r u", b=2),
+                in_=t_banks[p][:].rearrange("p b u r -> p b r u"),
+            )
+            n_grouped[p] = grouped
+
+        def quantize_n(p):
+            codes = stage.tile([P, PAIR], U32, name="n_codes", bufs=2, align_bytes=64)
+            planes = stage.tile([P, PAIR], U8, name="n_planes", bufs=2, align_bytes=64)
+            nc.vector.quantize_mx(
+                out=codes[:].bitcast(FP8X4), scales=planes[:], in_=n_grouped[p][:].rearrange("p c t -> p (c t)")
+            )
+            n_codes[p], n_planes[p] = codes, planes
+
+        def second_bank(p):
+            bank = psum.tile([P, 2, 2 * G], F32, name="ri2_bank", tag="tr", bufs=1)
+            for b in range(2):
+                cols = slice(b * P, b * P + P)
+                nc.tensor.matmul_mx(
+                    out=bank[:, b, :],
+                    lhsT=n_codes[p][:, cols].bitcast(FP8X4),
+                    lhsT_scale=n_planes[p][:, cols],
+                    rhs=w2_codes[:, 0 : 2 * G].bitcast(FP8X4),
+                    rhs_scale=w2_planes[:, 0 : 2 * G],
+                    start=True,
+                    stop=True,
+                )
+            ri2_banks[p] = bank
+
+        def first_order(p):
+            bank = psum.tile([P, 2, PAIR], F32, name="o_bank", tag="o", bufs=1)
+            nc.tensor.matmul_mx(
+                out=bank[:, 0, :],
+                lhsT=w2_codes[:, 2 * G : 3 * G].bitcast(FP8X4),
+                lhsT_scale=w2_planes[:, 2 * G : 3 * G],
+                rhs=n_codes[p][:].bitcast(FP8X4),
+                rhs_scale=n_planes[p][:],
+                start=True,
+                stop=True,
+            )
+            o_banks[p] = bank
+
+        def store_s1(p):
+            s1 = stage.tile([P, PAIR], F32, name="s1", bufs=3)
+            nc.vector.tensor_copy(out=s1[:], in_=o_banks[p][:, 0, :])
+            nc.sync.dma_start(out=out_0[:, p * PAIR : p * PAIR + PAIR], in_=s1[:])
+
+        def square2(p):
+            sq = stage.tile([P, 2, 2, G], F32, name="square2", bufs=2)
+            nc.scalar.activation(
+                out=sq[:].rearrange("p b i g -> p (b i g)"),
+                in_=ri2_banks[p][:].rearrange("p b n -> p (b n)"),
+                func=ACT.Square,
+            )
+            squares2[p] = sq
+
+        def add_turned2(p):
+            for b in range(2):
+                for i in range(2):
+                    nc.tensor.matmul(
+                        out=o_banks[p][:, 1, b * P : b * P + P],
+                        lhsT=squares2[p][:, b, i, :],
+                        rhs=ident[:],
+                        is_transpose=True,
+                        start=(i == 0),
+                        stop=(i == 1),
+                    )
+
+        def store_u2(p):
+            u2 = stage.tile([P, PAIR], F32, name="u2", bufs=3)
+            nc.scalar.activation(out=u2[:], in_=o_banks[p][:, 1, :], func=ACT.Sqrt, bias=quarter[:, 0:1])
+            nc.sync.dma_start(out=out_1[:, p * PAIR : p * PAIR + PAIR], in_=u2[:])
+
+        widen(0)
+        group(0, 0)
+        group(0, 1)
+        quantize_x(0)
+        for u in range(2):
+            for n in ("ar", "aim"):
+                group_a(n, u, turn_a(n, u))
+        quantize_a("ar", 0)
+        quantize_a("aim", 0)
+        widen(1)
+        quantize_a("ar", 1)
+        quantize_a("aim", 1)
+        for ft in range(3):
+            first_bank(0, ft)
+        turn_w2()
+        group_w2()
+        group(1, 0)
+        group(1, 1)
+        widen(2)
+        quantize_x(1)
+        gain = keep.tile([P, F], F32, name="gain")
+        nc.gpsimd.tensor_copy(
+            out=gain[:].rearrange("p (u q e) -> p u q e", u=2, e=2),
+            in_=g_plain[:].rearrange("p (q u e) -> p u q e", u=2, e=2),
+        )
+        gains.append(gain)
+        group(2, 0)
+        group(2, 1)
+        quantize_w2()
+        widen(3)
+        quantize_x(2)
+
+        def live(p):
+            return 0 <= p < N_PAIRS
+
+        def chunk_at(p, ahead):
+            k = (p + ahead) // 2
+            return k if (p + ahead) % 2 == 0 and k < len(CHUNKS) else 0
+
+        for p in range(N_PAIRS + 4):
+            if live(p - 3):
+                store_u2(p - 3)
+            for ft in range(3):
+                if live(p):
+                    square(p, ft)
+            if live(p - 2):
+                group_n(p - 2)
+            if chunk_at(p, 6):
+                group(chunk_at(p, 6), 0)
+            if p >= 1 and chunk_at(p, 5):
+                quantize_x(chunk_at(p, 5))
+            if live(p - 2):
+                quantize_n(p - 2)
+            if chunk_at(p, 6):
+                group(chunk_at(p, 6), 1)
+            if chunk_at(p, 7):
+                widen(chunk_at(p, 7))
+            if live(p):
+                first_bank(p, 3)
+            if live(p + 1):
+                first_bank(p + 1, 0)
+                first_bank(p + 1, 1)
+            if live(p - 2):
+                second_bank(p - 2)
+                first_order(p - 2)
+            if live(p + 1):
+                first_bank(p + 1, 2)
+            if live(p - 1):
+                modulus(p - 1)
+            if live(p - 2):
+                square2(p - 2)
+                store_s1(p - 2)
+            if live(p):
+                square(p, 3)
+            if live(p - 1):
+                centre(p - 1)
+            if live(p):
+                open_c(p)
+                for b in range(2):
+                    add_turned(p, b, range(3))
+            if live(p - 2):
+                add_turned2(p - 2)
+            if live(p - 1):
+                turn_n(p - 1)
+            if live(p):
+                for b in range(2):
+                    add_turned(p, b, range(3, N_FT))

@@ -99,7 +99,8 @@ def tile_learnedsecondorderscattering_t_kernel(
                 x_grouped[k] = grouped
             cols = slice(half * n // 2, (half + 1) * n // 2)
             nc.vector.tensor_copy(
-                out=x_grouped[k][:, cols, :], in_=x_wide[k][:, :, cols].rearrange("p t c -> p c t")
+                out=x_grouped[k][:, cols, :].rearrange("p (c i) t -> p c t i", i=4),
+                in_=x_wide[k][:, :, cols].rearrange("p t (c i) -> p c t i", i=4),
             )
 
         def quantize_x(k):
@@ -169,7 +170,7 @@ def tile_learnedsecondorderscattering_t_kernel(
                 )
 
         sq_banks, squares, c_banks, gains = {}, {}, {}, []
-        u1s, means, n1s, t_banks, n_grouped, n_codes, n_planes = {}, {}, {}, {}, {}, {}, {}
+        u1s, totals, means, n1s, t_banks, n_grouped, n_codes, n_planes = {}, {}, {}, {}, {}, {}, {}, {}
         ri2_banks, o_banks, squares2 = {}, {}, {}
 
         def where(p):
@@ -220,15 +221,19 @@ def tile_learnedsecondorderscattering_t_kernel(
                     )
 
         def modulus(p):
+            total = stage.tile([P, 2], F32, name="total", bufs=4)
+            totals[p] = total
             for b in range(2):
-                total = stage.tile([P, 1], F32, name="total", bufs=6)
-                mean = stage.tile([P, 1], F32, name="mean", bufs=6)
-                u1 = stage.tile([P, F], F32, name="u1", bufs=4)
+                u1 = stage.tile([P, F], F32, name="u1", bufs=6)
                 nc.scalar.activation(
-                    out=u1[:], in_=c_banks[p][b][:], func=ACT.Sqrt, bias=quarter[:, 0:1], accum_out=total[:, 0:1]
+                    out=u1[:], in_=c_banks[p][b][:], func=ACT.Sqrt, bias=quarter[:, 0:1], accum_out=total[:, b : b + 1]
                 )
-                nc.gpsimd.tensor_scalar(out=mean[:], in0=total[:], scalar1=1.0 / F, scalar2=None, op0=ALU.mult)
-                u1s[p, b], means[p, b] = u1, mean
+                u1s[p, b] = u1
+
+        def average(p):
+            mean = stage.tile([P, 2], F32, name="mean", bufs=4)
+            nc.vector.tensor_scalar(out=mean[:], in0=totals[p][:], scalar1=1.0 / F, scalar2=None, op0=ALU.mult)
+            means[p] = mean
 
         def centre(p):
             n1s[p] = []
@@ -237,7 +242,7 @@ def tile_learnedsecondorderscattering_t_kernel(
                 nc.vector.scalar_tensor_tensor(
                     out=n1[:],
                     in0=u1s[p, b][:],
-                    scalar=means[p, b][:, 0:1],
+                    scalar=means[p][:, b : b + 1],
                     in1=gains[0][:],
                     op0=ALU.subtract,
                     op1=ALU.mult,
@@ -261,8 +266,8 @@ def tile_learnedsecondorderscattering_t_kernel(
             n_grouped[p] = grouped
 
         def quantize_n(p):
-            codes = stage.tile([P, PAIR], U32, name="n_codes", bufs=2, align_bytes=64)
-            planes = stage.tile([P, PAIR], U8, name="n_planes", bufs=2, align_bytes=64)
+            codes = stage.tile([P, PAIR], U32, name="n_codes", bufs=3, align_bytes=64)
+            planes = stage.tile([P, PAIR], U8, name="n_planes", bufs=3, align_bytes=64)
             nc.vector.quantize_mx(
                 out=codes[:].bitcast(FP8X4), scales=planes[:], in_=n_grouped[p][:].rearrange("p c t -> p (c t)")
             )
@@ -339,8 +344,8 @@ def tile_learnedsecondorderscattering_t_kernel(
         widen(1)
         quantize_a("ar", 1)
         quantize_a("aim", 1)
-        for ft in range(3):
-            first_bank(0, ft)
+        first_bank(0, 0)
+        first_bank(0, 1)
         turn_w2()
         group_w2()
         group(1, 0)
@@ -366,51 +371,54 @@ def tile_learnedsecondorderscattering_t_kernel(
             k = (p + ahead) // 2
             return k if (p + ahead) % 2 == 0 and k < len(CHUNKS) else 0
 
-        for p in range(N_PAIRS + 4):
+        for p in range(N_PAIRS + 5):
+            if live(p):
+                square(p, 0)
+            if live(p - 5):
+                store_u2(p - 5)
+            if live(p):
+                square(p, 1)
             if live(p - 3):
-                store_u2(p - 3)
-            for ft in range(3):
-                if live(p):
-                    square(p, ft)
-            if live(p - 2):
-                group_n(p - 2)
+                group_n(p - 3)
             if chunk_at(p, 6):
                 group(chunk_at(p, 6), 0)
             if p >= 1 and chunk_at(p, 5):
                 quantize_x(chunk_at(p, 5))
+            if live(p - 3):
+                quantize_n(p - 3)
             if live(p - 2):
-                quantize_n(p - 2)
+                centre(p - 2)
             if chunk_at(p, 6):
                 group(chunk_at(p, 6), 1)
             if chunk_at(p, 7):
                 widen(chunk_at(p, 7))
+            if live(p - 4):
+                second_bank(p - 4)
+                first_order(p - 4)
             if live(p):
+                first_bank(p, 2)
                 first_bank(p, 3)
             if live(p + 1):
                 first_bank(p + 1, 0)
                 first_bank(p + 1, 1)
-            if live(p - 2):
-                second_bank(p - 2)
-                first_order(p - 2)
-            if live(p + 1):
-                first_bank(p + 1, 2)
             if live(p - 1):
                 modulus(p - 1)
-            if live(p - 2):
-                square2(p - 2)
-                store_s1(p - 2)
-            if live(p):
-                square(p, 3)
+            if live(p - 4):
+                square2(p - 4)
+                store_s1(p - 4)
             if live(p - 1):
-                centre(p - 1)
+                average(p - 1)
             if live(p):
+                square(p, 2)
+                square(p, 3)
                 open_c(p)
                 for b in range(2):
-                    add_turned(p, b, range(3))
+                    add_turned(p, b, range(2))
+            if live(p - 4):
+                add_turned2(p - 4)
             if live(p - 2):
-                add_turned2(p - 2)
-            if live(p - 1):
-                turn_n(p - 1)
+                turn_n(p - 2)
             if live(p):
-                for b in range(2):
-                    add_turned(p, b, range(3, N_FT))
+                for ft in range(2, N_FT):
+                    for b in range(2):
+                        add_turned(p, b, range(ft, ft + 1))

@@ -20,6 +20,7 @@ P = 128
 PAIR = 256
 N_PAIRS = C // PAIR
 N_FT = F // P
+ORDER = [["q",0,0],["a",7,1],["f",2,0],["g",0,3],["f",0,-1],["r",0,4],["q",1,0],["z",0,5],["m",0,1],["o",0,4],["c",0,2],["q",2,0],["w",0,4],["n",0,3],["f",1,-1],["m",1,1],["c",1,2],["f",3,0],["s",0,4],["x",0,0],["a",0,0],["a",2,0],["a",1,0],["t",0,2],["t",1,2],["q",3,0],["b",0,4],["a",4,0],["a",6,0],["a",5,0],["x",1,0],["v",0,1],["a",3,0]]
 CHUNKS = [256, 256] + [512] * 11
 LOADS = [256, 256, 512, 1024, 1024, 1024, 1024, 1024]
 
@@ -47,25 +48,29 @@ def tile_learnedsecondorderscattering_t_kernel(
             nc.sync.dma_start(out=xb[:], in_=x_rows[:, :, first : first + LOADS[i]])
             x_at.append((first, first + LOADS[i], xb))
 
+        bank_rows = {}
+
+        def load_a(name, w, u):
+            rows = keep.tile([P, 2, S], BF16, name=f"{name}_rows{u}", align_bytes=64)
+            nc.sync.dma_start(
+                out=rows[:], in_=w.rearrange("(q s) k -> q s k", s=4)[:, 2 * u : 2 * u + 2, :]
+            )
+            bank_rows[name, u] = rows
+
+        load_a("ar", ar, 0)
         load_x(0)
+        load_a("aim", aim, 0)
+        load_a("ar", ar, 1)
+        load_a("aim", aim, 1)
+        load_x(1)
+        load_x(2)
         quarter = keep.tile([P, 1], F32, name="quarter")
         nc.vector.memset(quarter[:], 0.25)
         warm = keep.tile([P, 1], F32, name="warm")
         nc.scalar.activation(out=warm[:], in_=quarter[:], func=ACT.Sqrt)
-
-        bank_rows = {}
-        for u in range(2):
-            for name, w in (("ar", ar), ("aim", aim)):
-                rows = keep.tile([P, 2, S], BF16, name=f"{name}_rows{u}", align_bytes=64)
-                nc.sync.dma_start(
-                    out=rows[:], in_=w.rearrange("(q s) k -> q s k", s=4)[:, 2 * u : 2 * u + 2, :]
-                )
-                bank_rows[name, u] = rows
-        load_x(1)
         w2_rows = keep.tile([P, 3, F], BF16, name="w2_rows", align_bytes=64)
         for m, w in enumerate((cr, cim, phi)):
             nc.sync.dma_start(out=w2_rows[:, m, :], in_=w)
-        load_x(2)
         g_plain = keep.tile([P, F], BF16, name="g_plain")
         nc.sync.dma_start(out=g_plain[:], in_=g1.partition_broadcast(P))
         for i in range(3, len(LOADS)):
@@ -126,8 +131,8 @@ def tile_learnedsecondorderscattering_t_kernel(
                     nc.tensor.transpose(turned[:, e, v, :], words[:, v : S // 2 : 2], ident[:])
             return turned
 
-        def group_a(name, u, turned):
-            nc.scalar.copy(
+        def group_a(name, u, turned, copy):
+            copy(
                 out=a_grouped[name][:, u * 256 : u * 256 + 256, :].bitcast(F32).rearrange("p (q e) v -> p q e v", e=2),
                 in_=turned[:].rearrange("p e v q -> p q e v"),
             )
@@ -147,7 +152,7 @@ def tile_learnedsecondorderscattering_t_kernel(
 
         def turn_w2():
             for ms in ((0, 1), (2,)):
-                turned = psum.tile([P, 2, 2, P], F32, name="turned2", tag="c", bufs=2)
+                turned = psum.tile([P, 2, 2, P], F32, name="turned2", tag="tr" if ms[0] == 0 else "o", bufs=1)
                 for i, m in enumerate(ms):
                     words = w2_rows[:, m, :].bitcast(F32)
                     for v in range(2):
@@ -198,67 +203,66 @@ def tile_learnedsecondorderscattering_t_kernel(
             sq_banks[p, ft] = bank
 
         def square(p, ft):
-            sq = stage.tile([P, 2, PAIR], F32, name="square", bufs=10)
+            sq = stage.tile([P, 2, PAIR], F32, name="square", bufs=12)
             nc.scalar.activation(out=sq[:], in_=sq_banks[p, ft][:], func=ACT.Square)
             squares[p, ft] = sq
 
-        def open_c(p):
-            c_banks[p] = []
-            for b in range(2):
+        def add_turned(p, bft):
+            b, ft = bft // 4, bft % 4
+            if ft == 0:
                 bank = psum.tile([P, F], F32, name="c_bank", tag="c", bufs=2)
-                c_banks[p].append(bank)
-
-        def add_turned(p, b, fts):
-            for ft in fts:
-                for i in range(2):
-                    nc.tensor.matmul(
-                        out=c_banks[p][b][:, ft * P : ft * P + P],
-                        lhsT=squares[p, ft][:, i, b * P : b * P + P],
-                        rhs=ident[:],
-                        is_transpose=True,
-                        start=(i == 0),
-                        stop=(i == 1),
-                    )
-
-        def modulus(p):
-            total = stage.tile([P, 2], F32, name="total", bufs=4)
-            totals[p] = total
-            for b in range(2):
-                u1 = stage.tile([P, F], F32, name="u1", bufs=6)
-                nc.scalar.activation(
-                    out=u1[:], in_=c_banks[p][b][:], func=ACT.Sqrt, bias=quarter[:, 0:1], accum_out=total[:, b : b + 1]
+                c_banks[p, b] = bank
+            for i in range(2):
+                nc.tensor.matmul(
+                    out=c_banks[p, b][:, ft * P : ft * P + P],
+                    lhsT=squares[p, ft][:, i, b * P : b * P + P],
+                    rhs=ident[:],
+                    is_transpose=True,
+                    start=(i == 0),
+                    stop=(i == 1),
                 )
-                u1s[p, b] = u1
+
+        def modulus(p, b):
+            if b == 0:
+                total = stage.tile([P, 2], F32, name="total", bufs=6)
+                totals[p] = total
+            u1 = stage.tile([P, F], F32, name="u1", bufs=8)
+            nc.scalar.activation(
+                out=u1[:],
+                in_=c_banks[p, b][:],
+                func=ACT.Sqrt,
+                bias=quarter[:, 0:1],
+                accum_out=totals[p][:, b : b + 1],
+            )
+            u1s[p, b] = u1
 
         def average(p):
-            mean = stage.tile([P, 2], F32, name="mean", bufs=4)
+            mean = stage.tile([P, 2], F32, name="mean", bufs=6)
             nc.vector.tensor_scalar(out=mean[:], in0=totals[p][:], scalar1=1.0 / F, scalar2=None, op0=ALU.mult)
             means[p] = mean
 
-        def centre(p):
-            n1s[p] = []
-            for b in range(2):
-                n1 = stage.tile([P, F], BF16, name="n1", bufs=4, align_bytes=64)
-                nc.vector.scalar_tensor_tensor(
-                    out=n1[:],
-                    in0=u1s[p, b][:],
-                    scalar=means[p][:, b : b + 1],
-                    in1=gains[0][:],
-                    op0=ALU.subtract,
-                    op1=ALU.mult,
-                )
-                n1s[p].append(n1)
+        def centre(p, b):
+            n1 = stage.tile([P, F], BF16, name="n1", bufs=6, align_bytes=64)
+            nc.vector.scalar_tensor_tensor(
+                out=n1[:],
+                in0=u1s[p, b][:],
+                scalar=means[p][:, b : b + 1],
+                in1=gains[0][:],
+                op0=ALU.subtract,
+                op1=ALU.mult,
+            )
+            n1s[p, b] = n1
 
-        def turn_n(p):
-            bank = psum.tile([P, 2, 2, P], F32, name="t_bank", tag="tr", bufs=1)
-            for b in range(2):
-                words = n1s[p][b][:].bitcast(F32)
-                for u in range(2):
-                    nc.tensor.transpose(bank[:, b, u, :], words[:, u * P : u * P + P], ident[:])
-            t_banks[p] = bank
+        def turn_n(p, b):
+            if b == 0:
+                bank = psum.tile([P, 2, 2, P], F32, name="t_bank", tag="tr", bufs=1)
+                t_banks[p] = bank
+            words = n1s[p, b][:].bitcast(F32)
+            for u in range(2):
+                nc.tensor.transpose(t_banks[p][:, b, u, :], words[:, u * P : u * P + P], ident[:])
 
         def group_n(p):
-            grouped = stage.tile([P, PAIR, 4], BF16, name="n_grouped", bufs=2, align_bytes=64)
+            grouped = stage.tile([P, PAIR, 4], BF16, name="n_grouped", bufs=3, align_bytes=64)
             nc.vector.tensor_copy(
                 out=grouped[:].bitcast(F32).rearrange("p (b r) u -> p b r u", b=2),
                 in_=t_banks[p][:].rearrange("p b u r -> p b r u"),
@@ -266,8 +270,8 @@ def tile_learnedsecondorderscattering_t_kernel(
             n_grouped[p] = grouped
 
         def quantize_n(p):
-            codes = stage.tile([P, PAIR], U32, name="n_codes", bufs=3, align_bytes=64)
-            planes = stage.tile([P, PAIR], U8, name="n_planes", bufs=3, align_bytes=64)
+            codes = stage.tile([P, PAIR], U32, name="n_codes", bufs=4, align_bytes=64)
+            planes = stage.tile([P, PAIR], U8, name="n_planes", bufs=4, align_bytes=64)
             nc.vector.quantize_mx(
                 out=codes[:].bitcast(FP8X4), scales=planes[:], in_=n_grouped[p][:].rearrange("p c t -> p (c t)")
             )
@@ -307,7 +311,7 @@ def tile_learnedsecondorderscattering_t_kernel(
             nc.sync.dma_start(out=out_0[:, p * PAIR : p * PAIR + PAIR], in_=s1[:])
 
         def square2(p):
-            sq = stage.tile([P, 2, 2, G], F32, name="square2", bufs=2)
+            sq = stage.tile([P, 2, 2, G], F32, name="square2", bufs=3)
             nc.scalar.activation(
                 out=sq[:].rearrange("p b i g -> p (b i g)"),
                 in_=ri2_banks[p][:].rearrange("p b n -> p (b n)"),
@@ -332,25 +336,27 @@ def tile_learnedsecondorderscattering_t_kernel(
             nc.scalar.activation(out=u2[:], in_=o_banks[p][:, 1, :], func=ACT.Sqrt, bias=quarter[:, 0:1])
             nc.sync.dma_start(out=out_1[:, p * PAIR : p * PAIR + PAIR], in_=u2[:])
 
+        turned_ar0 = turn_a("ar", 0)
+        group_a("ar", 0, turned_ar0, nc.scalar.copy)
         widen(0)
         group(0, 0)
         group(0, 1)
-        quantize_x(0)
-        for u in range(2):
-            for n in ("ar", "aim"):
-                group_a(n, u, turn_a(n, u))
         quantize_a("ar", 0)
+        quantize_x(0)
+        turned_aim0 = turn_a("aim", 0)
+        group_a("aim", 0, turned_aim0, nc.scalar.copy)
         quantize_a("aim", 0)
         widen(1)
+        turned_ar1 = turn_a("ar", 1)
+        group_a("ar", 1, turned_ar1, nc.scalar.copy)
         quantize_a("ar", 1)
-        quantize_a("aim", 1)
+        turned_aim1 = turn_a("aim", 1)
+        group_a("aim", 1, turned_aim1, nc.scalar.copy)
         first_bank(0, 0)
         first_bank(0, 1)
-        turn_w2()
-        group_w2()
         group(1, 0)
         group(1, 1)
-        widen(2)
+        quantize_a("aim", 1)
         quantize_x(1)
         gain = keep.tile([P, F], F32, name="gain")
         nc.gpsimd.tensor_copy(
@@ -358,67 +364,35 @@ def tile_learnedsecondorderscattering_t_kernel(
             in_=g_plain[:].rearrange("p (q u e) -> p u q e", u=2, e=2),
         )
         gains.append(gain)
+        widen(2)
         group(2, 0)
         group(2, 1)
-        quantize_w2()
-        widen(3)
-        quantize_x(2)
 
-        def live(p):
-            return 0 <= p < N_PAIRS
+        def x_part(p, half):
+            if p % 2 == 1:
+                if (p + 5) // 2 < len(CHUNKS):
+                    group((p + 5) // 2, half)
+            elif half == 0:
+                if (p + 4) // 2 < len(CHUNKS):
+                    quantize_x((p + 4) // 2)
+            elif (p + 6) // 2 < len(CHUNKS):
+                widen((p + 6) // 2)
 
-        def chunk_at(p, ahead):
-            k = (p + ahead) // 2
-            return k if (p + ahead) % 2 == 0 and k < len(CHUNKS) else 0
-
-        for p in range(N_PAIRS + 5):
-            if live(p):
-                square(p, 0)
-            if live(p - 5):
-                store_u2(p - 5)
-            if live(p):
-                square(p, 1)
-            if live(p - 3):
-                group_n(p - 3)
-            if chunk_at(p, 6):
-                group(chunk_at(p, 6), 0)
-            if p >= 1 and chunk_at(p, 5):
-                quantize_x(chunk_at(p, 5))
-            if live(p - 3):
-                quantize_n(p - 3)
-            if live(p - 2):
-                centre(p - 2)
-            if chunk_at(p, 6):
-                group(chunk_at(p, 6), 1)
-            if chunk_at(p, 7):
-                widen(chunk_at(p, 7))
-            if live(p - 4):
-                second_bank(p - 4)
-                first_order(p - 4)
-            if live(p):
-                first_bank(p, 2)
-                first_bank(p, 3)
-            if live(p + 1):
-                first_bank(p + 1, 0)
-                first_bank(p + 1, 1)
-            if live(p - 1):
-                modulus(p - 1)
-            if live(p - 4):
-                square2(p - 4)
-                store_s1(p - 4)
-            if live(p - 1):
-                average(p - 1)
-            if live(p):
-                square(p, 2)
-                square(p, 3)
-                open_c(p)
-                for b in range(2):
-                    add_turned(p, b, range(2))
-            if live(p - 4):
-                add_turned2(p - 4)
-            if live(p - 2):
-                turn_n(p - 2)
-            if live(p):
-                for ft in range(2, N_FT):
-                    for b in range(2):
-                        add_turned(p, b, range(ft, ft + 1))
+        steps = {
+            "q": square, "f": first_bank, "a": add_turned, "m": modulus, "c": centre, "t": turn_n,
+            "x": x_part, "v": lambda p, j: average(p), "g": lambda p, j: group_n(p), "n": lambda p, j: quantize_n(p),
+            "r": lambda p, j: second_bank(p), "o": lambda p, j: first_order(p), "s": lambda p, j: store_s1(p),
+            "w": lambda p, j: square2(p), "b": lambda p, j: add_turned2(p), "z": lambda p, j: store_u2(p),
+        }
+        for p in range(N_PAIRS + 6):
+            if p == 1:
+                turn_w2()
+                group_w2()
+            if p == 2:
+                quantize_w2()
+            for name, j, lag in ORDER:
+                if name == "x":
+                    if p < N_PAIRS:
+                        steps[name](p, j)
+                elif 0 <= p - lag < N_PAIRS:
+                    steps[name](p - lag, j)

@@ -4,6 +4,7 @@ import concourse.mybir as mybir
 from concourse.masks import make_identity
 
 S, F, G, T, C = 512, 512, 128, 128, 6144
+FLOPS = 2 * C * (2 * F * S + 2 * G * F + T * F)
 
 F32 = mybir.dt.float32
 BF16 = mybir.dt.bfloat16
@@ -14,15 +15,13 @@ FP8X4 = mybir.dt.float8_e4m3fn_x4
 ACT = mybir.ActivationFunctionType
 ALU = mybir.AluOpType
 
-FLOPS = 2 * C * (2 * F * S + 2 * G * F + T * F)
-
 P = 128
-PAIR = 256
-N_PAIRS = C // PAIR
-N_FT = F // P
-ORDER = [["q",0,0],["a",7,1],["f",2,0],["g",0,3],["f",0,-1],["r",0,4],["q",1,0],["z",0,5],["m",0,1],["o",0,4],["c",0,2],["q",2,0],["w",0,4],["n",0,3],["f",1,-1],["m",1,1],["c",1,2],["f",3,0],["s",0,4],["x",0,0],["a",0,0],["a",2,0],["a",1,0],["t",0,2],["t",1,2],["q",3,0],["b",0,4],["a",4,0],["a",6,0],["a",5,0],["x",1,0],["v",0,1],["a",3,0]]
-CHUNKS = [256, 256] + [512] * 11
-LOADS = [256, 256, 512, 1024, 1024, 1024, 1024, 1024]
+BATCH = 256
+N_BATCHES = C // BATCH
+FILTER_TILES = F // P
+CHUNKS = [BATCH] * 2 + [2 * BATCH] * 11
+LOADS = [256, 256, 512] + [1024] * 5
+LATE = 4
 
 
 def tile_learnedsecondorderscattering_t_kernel(
@@ -37,72 +36,69 @@ def tile_learnedsecondorderscattering_t_kernel(
         make_identity(nc, ident[:])
         ctx.enter_context(tc.manual_schedule())
 
-        scale = keep.tile([P, 4], F32, name="scale")
-        nc.sync.dma_start(out=scale[:], in_=x_scale.rearrange("(p t) o -> p (t o)", t=4))
-        x_rows = x_bytes.rearrange("(p t) c -> p t c", t=4)
-        x_at = []
+        a_rows, x_loads = {}, []
 
-        def load_x(i):
-            first = sum(LOADS[:i])
-            xb = keep.tile([P, 4, LOADS[i]], U8, name=f"xb{i}", align_bytes=64)
-            nc.sync.dma_start(out=xb[:], in_=x_rows[:, :, first : first + LOADS[i]])
-            x_at.append((first, first + LOADS[i], xb))
-
-        bank_rows = {}
-
-        def load_a(name, w, u):
+        def load_a(name, weights, u):
             rows = keep.tile([P, 2, S], BF16, name=f"{name}_rows{u}", align_bytes=64)
             nc.sync.dma_start(
-                out=rows[:], in_=w.rearrange("(q s) k -> q s k", s=4)[:, 2 * u : 2 * u + 2, :]
+                out=rows[:], in_=weights.rearrange("(q s) k -> q s k", s=4)[:, 2 * u : 2 * u + 2, :]
             )
-            bank_rows[name, u] = rows
+            a_rows[name, u] = rows
 
+        def load_x():
+            i = len(x_loads)
+            first = sum(LOADS[:i])
+            codes_in = keep.tile([P, 4, LOADS[i]], U8, name=f"codes_in{i}", align_bytes=64)
+            nc.sync.dma_start(
+                out=codes_in[:],
+                in_=x_bytes.rearrange("(p t) c -> p t c", t=4)[:, :, first : first + LOADS[i]],
+            )
+            x_loads.append(codes_in)
+
+        scale = keep.tile([P, 4], F32, name="scale")
+        nc.sync.dma_start(out=scale[:], in_=x_scale.rearrange("(p t) o -> p (t o)", t=4))
         load_a("ar", ar, 0)
-        load_x(0)
+        load_x()
         load_a("aim", aim, 0)
         load_a("ar", ar, 1)
         load_a("aim", aim, 1)
-        load_x(1)
-        load_x(2)
+        load_x()
+        load_x()
+        w2_rows = keep.tile([P, 3, F], BF16, name="w2_rows", align_bytes=64)
+        for m, weights in enumerate((cr, cim, phi)):
+            nc.sync.dma_start(out=w2_rows[:, m, :], in_=weights)
+        gain_plain = keep.tile([P, F], BF16, name="gain_plain")
+        nc.sync.dma_start(out=gain_plain[:], in_=g1.partition_broadcast(P))
+        while len(x_loads) < len(LOADS):
+            load_x()
+
         quarter = keep.tile([P, 1], F32, name="quarter")
         nc.vector.memset(quarter[:], 0.25)
         warm = keep.tile([P, 1], F32, name="warm")
         nc.scalar.activation(out=warm[:], in_=quarter[:], func=ACT.Sqrt)
-        w2_rows = keep.tile([P, 3, F], BF16, name="w2_rows", align_bytes=64)
-        for m, w in enumerate((cr, cim, phi)):
-            nc.sync.dma_start(out=w2_rows[:, m, :], in_=w)
-        g_plain = keep.tile([P, F], BF16, name="g_plain")
-        nc.sync.dma_start(out=g_plain[:], in_=g1.partition_broadcast(P))
-        for i in range(3, len(LOADS)):
-            load_x(i)
 
-        x_wide, x_grouped, x_codes, x_planes = {}, {}, {}, {}
-
-        def chunk_first(k):
-            return sum(CHUNKS[:k])
+        x_wide, x_grouped, x_codes, x_scales = {}, {}, {}, {}
 
         def widen(k):
             n = CHUNKS[k]
-            first = chunk_first(k)
+            source, first = (x_loads[k], 0) if k < 3 else (x_loads[3 + (k - 3) // 2], (k - 3) % 2 * n)
             wide = stage.tile([P, 4, n], BF16, name="x_wide", align_bytes=64)
-            for lo, hi, xb in x_at:
-                if lo <= first < hi:
-                    for t in range(4):
-                        nc.vector.tensor_scalar(
-                            out=wide[:, t, :],
-                            in0=xb[:, t, first - lo : first - lo + n].bitcast(FP8),
-                            scalar1=scale[:, t : t + 1],
-                            scalar2=None,
-                            op0=ALU.mult,
-                        )
+            for t in range(4):
+                nc.vector.tensor_scalar(
+                    out=wide[:, t, :],
+                    in0=source[:, t, first : first + n].bitcast(FP8),
+                    scalar1=scale[:, t : t + 1],
+                    scalar2=None,
+                    op0=ALU.mult,
+                )
             x_wide[k] = wide
 
-        def group(k, half):
+        def group_x(k, side):
             n = CHUNKS[k]
-            if half == 0:
+            if side == 0:
                 grouped = stage.tile([P, n, 4], BF16, name="x_grouped", align_bytes=64)
                 x_grouped[k] = grouped
-            cols = slice(half * n // 2, (half + 1) * n // 2)
+            cols = slice(side * n // 2, (side + 1) * n // 2)
             nc.vector.tensor_copy(
                 out=x_grouped[k][:, cols, :].rearrange("p (c i) t -> p c t i", i=4),
                 in_=x_wide[k][:, :, cols].rearrange("p t (c i) -> p c t i", i=4),
@@ -111,288 +107,334 @@ def tile_learnedsecondorderscattering_t_kernel(
         def quantize_x(k):
             n = CHUNKS[k]
             codes = stage.tile([P, n], U32, name="x_codes", bufs=3, align_bytes=64)
-            planes = stage.tile([P, n], U8, name="x_planes", bufs=3, align_bytes=64)
+            scales = stage.tile([P, n], U8, name="x_scales", bufs=3, align_bytes=64)
             nc.vector.quantize_mx(
                 out=codes[:].bitcast(FP8X4),
-                scales=planes[:],
+                scales=scales[:],
                 in_=x_grouped[k][:].rearrange("p c t -> p (c t)"),
             )
-            x_codes[k], x_planes[k] = codes, planes
+            x_codes[k], x_scales[k] = codes, scales
 
-        a_grouped = {n: keep.tile([P, F, 4], BF16, name=f"{n}_grouped", align_bytes=64) for n in ("ar", "aim")}
-        a_codes = {n: keep.tile([P, F], U32, name=f"{n}_codes", align_bytes=64) for n in ("ar", "aim")}
-        a_planes = {n: keep.tile([P, F], U8, name=f"{n}_planes", align_bytes=64) for n in ("ar", "aim")}
+        def prepare_x(p, side):
+            if p % 2 == 1:
+                if (p + 5) // 2 < len(CHUNKS):
+                    group_x((p + 5) // 2, side)
+            elif side == 0:
+                if (p + 4) // 2 < len(CHUNKS):
+                    quantize_x((p + 4) // 2)
+            elif (p + 6) // 2 < len(CHUNKS):
+                widen((p + 6) // 2)
+
+        a_grouped, a_codes, a_scales = {}, {}, {}
+        for name in ("ar", "aim"):
+            grouped = keep.tile([P, F, 4], BF16, name=f"{name}_grouped", align_bytes=64)
+            codes = keep.tile([P, F], U32, name=f"{name}_codes", align_bytes=64)
+            scales = keep.tile([P, F], U8, name=f"{name}_scales", align_bytes=64)
+            a_grouped[name], a_codes[name], a_scales[name] = grouped, codes, scales
 
         def turn_a(name, u):
-            turned = psum.tile([P, 2, 2, P], F32, name="turned", tag="sq", bufs=4)
+            turned = psum.tile([P, 2, 2, P], F32, name="turned_a", tag="sq", bufs=4)
             for e in range(2):
-                words = bank_rows[name, u][:, e, :].bitcast(F32)
+                words = a_rows[name, u][:, e, :].bitcast(F32)
                 for v in range(2):
                     nc.tensor.transpose(turned[:, e, v, :], words[:, v : S // 2 : 2], ident[:])
             return turned
 
-        def group_a(name, u, turned, copy):
-            copy(
-                out=a_grouped[name][:, u * 256 : u * 256 + 256, :].bitcast(F32).rearrange("p (q e) v -> p q e v", e=2),
+        def group_a(name, u, turned):
+            slots = slice(256 * u, 256 * u + 256)
+            nc.scalar.copy(
+                out=a_grouped[name][:, slots, :].bitcast(F32).rearrange("p (q e) v -> p q e v", e=2),
                 in_=turned[:].rearrange("p e v q -> p q e v"),
             )
 
         def quantize_a(name, u):
-            cols = slice(u * 256, u * 256 + 256)
+            slots = slice(256 * u, 256 * u + 256)
             nc.vector.quantize_mx(
-                out=a_codes[name][:, cols].bitcast(FP8X4),
-                scales=a_planes[name][:, cols],
-                in_=a_grouped[name][:, cols, :].rearrange("p j t -> p (j t)"),
+                out=a_codes[name][:, slots].bitcast(FP8X4),
+                scales=a_scales[name][:, slots],
+                in_=a_grouped[name][:, slots, :].rearrange("p j t -> p (j t)"),
             )
 
         w2_grouped = keep.tile([P, 3, P, 4], BF16, name="w2_grouped", align_bytes=64)
         w2_codes = keep.tile([P, 3 * P], U32, name="w2_codes", align_bytes=64)
-        w2_planes = keep.tile([P, 3 * P], U8, name="w2_planes", align_bytes=64)
-        w2_turned = []
+        w2_scales = keep.tile([P, 3 * P], U8, name="w2_scales", align_bytes=64)
 
-        def turn_w2():
-            for ms in ((0, 1), (2,)):
-                turned = psum.tile([P, 2, 2, P], F32, name="turned2", tag="tr" if ms[0] == 0 else "o", bufs=1)
-                for i, m in enumerate(ms):
-                    words = w2_rows[:, m, :].bitcast(F32)
-                    for v in range(2):
-                        nc.tensor.transpose(turned[:, i, v, :], words[:, v : F // 2 : 2], ident[:])
-                w2_turned.append((ms, turned))
+        def turn_and_group_w2(first, count, tag):
+            turned = psum.tile([P, 2, 2, P], F32, name="turned_w2", tag=tag, bufs=1)
+            for i in range(count):
+                words = w2_rows[:, first + i, :].bitcast(F32)
+                for v in range(2):
+                    nc.tensor.transpose(turned[:, i, v, :], words[:, v : F // 2 : 2], ident[:])
+            nc.vector.tensor_copy(
+                out=w2_grouped[:, first : first + count, :, :].bitcast(F32),
+                in_=turned[:, 0:count, :, :].rearrange("p m v g -> p m g v"),
+            )
 
-        def group_w2():
-            for ms, turned in w2_turned:
-                nc.vector.tensor_copy(
-                    out=w2_grouped[:, ms[0] : ms[-1] + 1, :, :].bitcast(F32),
-                    in_=turned[:, 0 : len(ms), :, :].rearrange("p m v g -> p m g v"),
-                )
+        def quantize_w2(first, count):
+            cols = slice(first * P, (first + count) * P)
+            nc.vector.quantize_mx(
+                out=w2_codes[:, cols].bitcast(FP8X4),
+                scales=w2_scales[:, cols],
+                in_=w2_grouped[:, first : first + count, :, :].rearrange("p m g t -> p (m g t)"),
+            )
 
-        def quantize_w2():
-            for lo, hi in ((0, 2), (2, 3)):
-                nc.vector.quantize_mx(
-                    out=w2_codes[:, lo * P : hi * P].bitcast(FP8X4),
-                    scales=w2_planes[:, lo * P : hi * P],
-                    in_=w2_grouped[:, lo:hi, :, :].rearrange("p m g t -> p (m g t)"),
-                )
+        gain = keep.tile([P, F], F32, name="gain")
 
-        sq_banks, squares, c_banks, gains = {}, {}, {}, []
-        u1s, totals, means, n1s, t_banks, n_grouped, n_codes, n_planes = {}, {}, {}, {}, {}, {}, {}, {}
-        ri2_banks, o_banks, squares2 = {}, {}, {}
+        def order_gain():
+            nc.gpsimd.tensor_copy(
+                out=gain[:].rearrange("p (u q e) -> p u q e", u=2, e=2),
+                in_=gain_plain[:].rearrange("p (q u e) -> p u q e", u=2, e=2),
+            )
 
-        def where(p):
-            c = p * PAIR
-            for k in range(len(CHUNKS)):
-                first = chunk_first(k)
-                if first <= c < first + CHUNKS[k]:
-                    return k, slice(c - first, c - first + PAIR)
-            raise AssertionError("no chunk")
+        ri1, squares, sums, u1s, totals, means = {}, {}, {}, {}, {}, {}
 
-        def first_bank(p, ft):
-            k, cols = where(p)
-            bank = psum.tile([P, 2, PAIR], F32, name="sq_bank", tag="sq", bufs=4)
-            rows = slice(ft * P, ft * P + P)
-            for i, n in enumerate(("ar", "aim")):
+        def first_bank(p, tile):
+            k, first = (p, 0) if p < 2 else (p // 2 + 1, p % 2 * BATCH)
+            cols = slice(first, first + BATCH)
+            slots = slice(tile * P, tile * P + P)
+            bank = psum.tile([P, 2, BATCH], F32, name="ri1", tag="sq", bufs=4)
+            for i, name in enumerate(("ar", "aim")):
                 nc.tensor.matmul_mx(
                     out=bank[:, i, :],
-                    lhsT=a_codes[n][:, rows].bitcast(FP8X4),
-                    lhsT_scale=a_planes[n][:, rows],
+                    lhsT=a_codes[name][:, slots].bitcast(FP8X4),
+                    lhsT_scale=a_scales[name][:, slots],
                     rhs=x_codes[k][:, cols].bitcast(FP8X4),
-                    rhs_scale=x_planes[k][:, cols],
+                    rhs_scale=x_scales[k][:, cols],
                     start=True,
                     stop=True,
                 )
-            sq_banks[p, ft] = bank
+            ri1[p, tile] = bank
 
-        def square(p, ft):
-            sq = stage.tile([P, 2, PAIR], F32, name="square", bufs=12)
-            nc.scalar.activation(out=sq[:], in_=sq_banks[p, ft][:], func=ACT.Square)
-            squares[p, ft] = sq
+        def square1(p, tile):
+            square = stage.tile([P, 2, BATCH], F32, name="square1", bufs=12)
+            nc.scalar.activation(out=square[:], in_=ri1[p, tile][:], func=ACT.Square)
+            squares[p, tile] = square
 
-        def add_turned(p, bft):
-            b, ft = bft // 4, bft % 4
-            if ft == 0:
-                bank = psum.tile([P, F], F32, name="c_bank", tag="c", bufs=2)
-                c_banks[p, b] = bank
+        def add_squares1(p, half, tile):
+            if tile == 0:
+                bank = psum.tile([P, F], F32, name="sum1", tag="c", bufs=2)
+                sums[p, half] = bank
             for i in range(2):
                 nc.tensor.matmul(
-                    out=c_banks[p, b][:, ft * P : ft * P + P],
-                    lhsT=squares[p, ft][:, i, b * P : b * P + P],
+                    out=sums[p, half][:, tile * P : tile * P + P],
+                    lhsT=squares[p, tile][:, i, half * P : half * P + P],
                     rhs=ident[:],
                     is_transpose=True,
                     start=(i == 0),
                     stop=(i == 1),
                 )
 
-        def modulus(p, b):
-            if b == 0:
+        def root1(p, half):
+            if half == 0:
                 total = stage.tile([P, 2], F32, name="total", bufs=6)
                 totals[p] = total
             u1 = stage.tile([P, F], F32, name="u1", bufs=8)
             nc.scalar.activation(
                 out=u1[:],
-                in_=c_banks[p, b][:],
+                in_=sums[p, half][:],
                 func=ACT.Sqrt,
                 bias=quarter[:, 0:1],
-                accum_out=totals[p][:, b : b + 1],
+                accum_out=totals[p][:, half : half + 1],
             )
-            u1s[p, b] = u1
+            u1s[p, half] = u1
 
         def average(p):
             mean = stage.tile([P, 2], F32, name="mean", bufs=6)
-            nc.vector.tensor_scalar(out=mean[:], in0=totals[p][:], scalar1=1.0 / F, scalar2=None, op0=ALU.mult)
+            nc.vector.tensor_scalar(
+                out=mean[:], in0=totals[p][:], scalar1=1.0 / F, scalar2=None, op0=ALU.mult
+            )
             means[p] = mean
 
-        def centre(p, b):
+        n1s, n1_turned, n1_grouped, n1_codes, n1_scales = {}, {}, {}, {}, {}
+
+        def centre(p, half):
             n1 = stage.tile([P, F], BF16, name="n1", bufs=6, align_bytes=64)
             nc.vector.scalar_tensor_tensor(
                 out=n1[:],
-                in0=u1s[p, b][:],
-                scalar=means[p][:, b : b + 1],
-                in1=gains[0][:],
+                in0=u1s[p, half][:],
+                scalar=means[p][:, half : half + 1],
+                in1=gain[:],
                 op0=ALU.subtract,
                 op1=ALU.mult,
             )
-            n1s[p, b] = n1
+            n1s[p, half] = n1
 
-        def turn_n(p, b):
-            if b == 0:
-                bank = psum.tile([P, 2, 2, P], F32, name="t_bank", tag="tr", bufs=1)
-                t_banks[p] = bank
-            words = n1s[p, b][:].bitcast(F32)
+        def turn_n1(p, half):
+            if half == 0:
+                bank = psum.tile([P, 2, 2, P], F32, name="n1_turned", tag="tr", bufs=1)
+                n1_turned[p] = bank
+            words = n1s[p, half][:].bitcast(F32)
             for u in range(2):
-                nc.tensor.transpose(t_banks[p][:, b, u, :], words[:, u * P : u * P + P], ident[:])
+                nc.tensor.transpose(n1_turned[p][:, half, u, :], words[:, u * P : u * P + P], ident[:])
 
-        def group_n(p):
-            grouped = stage.tile([P, PAIR, 4], BF16, name="n_grouped", bufs=3, align_bytes=64)
+        def group_n1(p):
+            grouped = stage.tile([P, BATCH, 4], BF16, name="n1_grouped", bufs=3, align_bytes=64)
             nc.vector.tensor_copy(
-                out=grouped[:].bitcast(F32).rearrange("p (b r) u -> p b r u", b=2),
-                in_=t_banks[p][:].rearrange("p b u r -> p b r u"),
+                out=grouped[:].bitcast(F32).rearrange("p (h r) u -> p h r u", h=2),
+                in_=n1_turned[p][:].rearrange("p h u r -> p h r u"),
             )
-            n_grouped[p] = grouped
+            n1_grouped[p] = grouped
 
-        def quantize_n(p):
-            codes = stage.tile([P, PAIR], U32, name="n_codes", bufs=4, align_bytes=64)
-            planes = stage.tile([P, PAIR], U8, name="n_planes", bufs=4, align_bytes=64)
+        def quantize_n1(p):
+            codes = stage.tile([P, BATCH], U32, name="n1_codes", bufs=4, align_bytes=64)
+            scales = stage.tile([P, BATCH], U8, name="n1_scales", bufs=4, align_bytes=64)
             nc.vector.quantize_mx(
-                out=codes[:].bitcast(FP8X4), scales=planes[:], in_=n_grouped[p][:].rearrange("p c t -> p (c t)")
+                out=codes[:].bitcast(FP8X4),
+                scales=scales[:],
+                in_=n1_grouped[p][:].rearrange("p c t -> p (c t)"),
             )
-            n_codes[p], n_planes[p] = codes, planes
+            n1_codes[p], n1_scales[p] = codes, scales
+
+        ri2, outs, squares2 = {}, {}, {}
 
         def second_bank(p):
-            bank = psum.tile([P, 2, 2 * G], F32, name="ri2_bank", tag="tr", bufs=1)
-            for b in range(2):
-                cols = slice(b * P, b * P + P)
+            late = p >= N_BATCHES - LATE
+            bank = psum.tile([P, 2, 2 * G], F32, name="ri2", tag="sq" if late else "tr", bufs=4 if late else 1)
+            for half in range(2):
+                cols = slice(half * P, half * P + P)
                 nc.tensor.matmul_mx(
-                    out=bank[:, b, :],
-                    lhsT=n_codes[p][:, cols].bitcast(FP8X4),
-                    lhsT_scale=n_planes[p][:, cols],
+                    out=bank[:, half, :],
+                    lhsT=n1_codes[p][:, cols].bitcast(FP8X4),
+                    lhsT_scale=n1_scales[p][:, cols],
                     rhs=w2_codes[:, 0 : 2 * G].bitcast(FP8X4),
-                    rhs_scale=w2_planes[:, 0 : 2 * G],
+                    rhs_scale=w2_scales[:, 0 : 2 * G],
                     start=True,
                     stop=True,
                 )
-            ri2_banks[p] = bank
+            ri2[p] = bank
 
         def first_order(p):
-            bank = psum.tile([P, 2, PAIR], F32, name="o_bank", tag="o", bufs=1)
+            late = p >= N_BATCHES - LATE
+            bank = psum.tile([P, 2, BATCH], F32, name="out", tag="sq" if late else "o", bufs=4 if late else 1)
             nc.tensor.matmul_mx(
                 out=bank[:, 0, :],
                 lhsT=w2_codes[:, 2 * G : 3 * G].bitcast(FP8X4),
-                lhsT_scale=w2_planes[:, 2 * G : 3 * G],
-                rhs=n_codes[p][:].bitcast(FP8X4),
-                rhs_scale=n_planes[p][:],
+                lhsT_scale=w2_scales[:, 2 * G : 3 * G],
+                rhs=n1_codes[p][:].bitcast(FP8X4),
+                rhs_scale=n1_scales[p][:],
                 start=True,
                 stop=True,
             )
-            o_banks[p] = bank
+            outs[p] = bank
 
         def store_s1(p):
-            s1 = stage.tile([P, PAIR], F32, name="s1", bufs=3)
-            nc.vector.tensor_copy(out=s1[:], in_=o_banks[p][:, 0, :])
-            nc.sync.dma_start(out=out_0[:, p * PAIR : p * PAIR + PAIR], in_=s1[:])
+            s1 = stage.tile([P, BATCH], F32, name="s1", bufs=3)
+            nc.vector.tensor_copy(out=s1[:], in_=outs[p][:, 0, :])
+            nc.sync.dma_start(out=out_0[:, p * BATCH : p * BATCH + BATCH], in_=s1[:])
 
         def square2(p):
-            sq = stage.tile([P, 2, 2, G], F32, name="square2", bufs=3)
-            nc.scalar.activation(
-                out=sq[:].rearrange("p b i g -> p (b i g)"),
-                in_=ri2_banks[p][:].rearrange("p b n -> p (b n)"),
-                func=ACT.Square,
-            )
-            squares2[p] = sq
+            square = stage.tile([P, 2, 2 * G], F32, name="square2", bufs=3)
+            nc.scalar.activation(out=square[:], in_=ri2[p][:], func=ACT.Square)
+            squares2[p] = square
 
-        def add_turned2(p):
-            for b in range(2):
+        def add_squares2(p):
+            for half in range(2):
                 for i in range(2):
                     nc.tensor.matmul(
-                        out=o_banks[p][:, 1, b * P : b * P + P],
-                        lhsT=squares2[p][:, b, i, :],
+                        out=outs[p][:, 1, half * P : half * P + P],
+                        lhsT=squares2[p][:, half, i * G : i * G + G],
                         rhs=ident[:],
                         is_transpose=True,
                         start=(i == 0),
                         stop=(i == 1),
                     )
 
-        def store_u2(p):
-            u2 = stage.tile([P, PAIR], F32, name="u2", bufs=3)
-            nc.scalar.activation(out=u2[:], in_=o_banks[p][:, 1, :], func=ACT.Sqrt, bias=quarter[:, 0:1])
-            nc.sync.dma_start(out=out_1[:, p * PAIR : p * PAIR + PAIR], in_=u2[:])
+        def late_add_squares2(p):
+            if p >= N_BATCHES - LATE:
+                add_squares2(p)
 
-        turned_ar0 = turn_a("ar", 0)
-        group_a("ar", 0, turned_ar0, nc.scalar.copy)
+        def store_u2(p):
+            u2 = stage.tile([P, BATCH], F32, name="u2", bufs=3)
+            nc.scalar.activation(out=u2[:], in_=outs[p][:, 1, :], func=ACT.Sqrt, bias=quarter[:, 0:1])
+            nc.sync.dma_start(out=out_1[:, p * BATCH : p * BATCH + BATCH], in_=u2[:])
+
+        turned = turn_a("ar", 0)
+        group_a("ar", 0, turned)
         widen(0)
-        group(0, 0)
-        group(0, 1)
+        group_x(0, 0)
+        group_x(0, 1)
         quantize_a("ar", 0)
         quantize_x(0)
-        turned_aim0 = turn_a("aim", 0)
-        group_a("aim", 0, turned_aim0, nc.scalar.copy)
+        turned = turn_a("aim", 0)
+        group_a("aim", 0, turned)
         quantize_a("aim", 0)
         widen(1)
-        turned_ar1 = turn_a("ar", 1)
-        group_a("ar", 1, turned_ar1, nc.scalar.copy)
+        turned = turn_a("ar", 1)
+        group_a("ar", 1, turned)
         quantize_a("ar", 1)
-        turned_aim1 = turn_a("aim", 1)
-        group_a("aim", 1, turned_aim1, nc.scalar.copy)
+        turned = turn_a("aim", 1)
+        group_a("aim", 1, turned)
+        group_x(1, 0)
+        quantize_a("aim", 1)
+        group_x(1, 1)
+        quantize_x(1)
+        order_gain()
+        widen(2)
+        group_x(2, 0)
+        group_x(2, 1)
         first_bank(0, 0)
         first_bank(0, 1)
-        group(1, 0)
-        group(1, 1)
-        quantize_a("aim", 1)
-        quantize_x(1)
-        gain = keep.tile([P, F], F32, name="gain")
-        nc.gpsimd.tensor_copy(
-            out=gain[:].rearrange("p (u q e) -> p u q e", u=2, e=2),
-            in_=g_plain[:].rearrange("p (q u e) -> p u q e", u=2, e=2),
-        )
-        gains.append(gain)
-        widen(2)
-        group(2, 0)
-        group(2, 1)
 
-        def x_part(p, half):
-            if p % 2 == 1:
-                if (p + 5) // 2 < len(CHUNKS):
-                    group((p + 5) // 2, half)
-            elif half == 0:
-                if (p + 4) // 2 < len(CHUNKS):
-                    quantize_x((p + 4) // 2)
-            elif (p + 6) // 2 < len(CHUNKS):
-                widen((p + 6) // 2)
-
-        steps = {
-            "q": square, "f": first_bank, "a": add_turned, "m": modulus, "c": centre, "t": turn_n,
-            "x": x_part, "v": lambda p, j: average(p), "g": lambda p, j: group_n(p), "n": lambda p, j: quantize_n(p),
-            "r": lambda p, j: second_bank(p), "o": lambda p, j: first_order(p), "s": lambda p, j: store_s1(p),
-            "w": lambda p, j: square2(p), "b": lambda p, j: add_turned2(p), "z": lambda p, j: store_u2(p),
-        }
-        for p in range(N_PAIRS + 6):
+        loop_order = [
+            (lambda p: add_squares1(p, 1, 3), 1),
+            (lambda p: square1(p, 0), 0),
+            (group_n1, 3),
+            (lambda p: first_bank(p, 2), 0),
+            (second_bank, 4),
+            (lambda p: first_bank(p, 3), 0),
+            (lambda p: square1(p, 1), 0),
+            (lambda p: centre(p, 0), 2),
+            (lambda p: centre(p, 1), 2),
+            (store_u2, 5),
+            (lambda p: root1(p, 0), 1),
+            (lambda p: square1(p, 2), 0),
+            (square2, 4),
+            (lambda p: root1(p, 1), 1),
+            (first_order, 4),
+            (lambda p: first_bank(p, 0), -1),
+            (quantize_n1, 3),
+            (lambda p: first_bank(p, 1), -1),
+            (lambda p: prepare_x(p, 0), 0),
+            (lambda p: add_squares1(p, 0, 0), 0),
+            (store_s1, 4),
+            (lambda p: add_squares1(p, 0, 1), 0),
+            (lambda p: square1(p, 3), 0),
+            (lambda p: add_squares1(p, 0, 2), 0),
+            (lambda p: turn_n1(p, 0), 2),
+            (lambda p: turn_n1(p, 1), 2),
+            (add_squares2, 4),
+            (lambda p: add_squares1(p, 1, 0), 0),
+            (lambda p: add_squares1(p, 1, 1), 0),
+            (lambda p: add_squares1(p, 1, 2), 0),
+            (lambda p: add_squares1(p, 0, 3), 0),
+            (lambda p: prepare_x(p, 1), 0),
+            (average, 1),
+        ]
+        drain_order = [
+            (lambda p: add_squares1(p, 1, 3), 1),
+            (second_bank, 4),
+            (first_order, 4),
+            (group_n1, 3),
+            (lambda p: root1(p, 0), 1),
+            (lambda p: centre(p, 0), 2),
+            (lambda p: centre(p, 1), 2),
+            (lambda p: root1(p, 1), 1),
+            (square2, 4),
+            (late_add_squares2, 5),
+            (lambda p: turn_n1(p, 0), 2),
+            (store_u2, 5),
+            (lambda p: turn_n1(p, 1), 2),
+            (quantize_n1, 3),
+            (store_s1, 4),
+            (average, 1),
+        ]
+        for p in range(N_BATCHES + 5):
             if p == 1:
-                turn_w2()
-                group_w2()
+                turn_and_group_w2(0, 2, "tr")
+                turn_and_group_w2(2, 1, "o")
             if p == 2:
-                quantize_w2()
-            for name, j, lag in ORDER:
-                if name == "x":
-                    if p < N_PAIRS:
-                        steps[name](p, j)
-                elif 0 <= p - lag < N_PAIRS:
-                    steps[name](p - lag, j)
+                quantize_w2(0, 2)
+                quantize_w2(2, 1)
+            for stage_of, behind in loop_order if p < N_BATCHES else drain_order:
+                if 0 <= p - behind < N_BATCHES:
+                    stage_of(p - behind)

from contextlib import ExitStack

import concourse.mybir as mybir
from concourse.masks import make_identity

S, F, G, T, C = 512, 512, 128, 128, 6144
FLOPS = 2 * C * (2 * F * S + 2 * G * F + T * F)

F32 = mybir.dt.float32
BF16 = mybir.dt.bfloat16
U32 = mybir.dt.uint32
U8 = mybir.dt.uint8
FP8 = mybir.dt.float8_e4m3fn
FP8X4 = mybir.dt.float8_e4m3fn_x4
ACT = mybir.ActivationFunctionType
ALU = mybir.AluOpType

P = 128
BATCH = 256
N_BATCHES = C // BATCH
FILTER_TILES = F // P
CHUNKS = [BATCH] * 2 + [2 * BATCH] * 11
LOADS = [256, 256, 512] + [1024] * 5
LATE = 4


def tile_learnedsecondorderscattering_t_kernel(
    tc, x_bytes, x_scale, ar, aim, g1, cr, cim, phi, out_0, out_1
):
    nc = tc.nc
    with ExitStack() as ctx:
        keep = ctx.enter_context(tc.tile_pool(name="keep", bufs=1))
        stage = ctx.enter_context(tc.tile_pool(name="stage", bufs=2))
        psum = ctx.enter_context(tc.psum_pool(name="psum", bufs=1))
        ident = keep.tile([P, P], F32, name="ident")
        make_identity(nc, ident[:])
        ctx.enter_context(tc.manual_schedule())

        a_rows, x_loads = {}, []

        def load_a(name, weights, u):
            rows = keep.tile([P, 2, S], BF16, name=f"{name}_rows{u}", align_bytes=64)
            nc.sync.dma_start(
                out=rows[:], in_=weights.rearrange("(q s) k -> q s k", s=4)[:, 2 * u : 2 * u + 2, :]
            )
            a_rows[name, u] = rows

        def load_x():
            i = len(x_loads)
            first = sum(LOADS[:i])
            codes_in = keep.tile([P, 4, LOADS[i]], U8, name=f"codes_in{i}", align_bytes=64)
            nc.sync.dma_start(
                out=codes_in[:],
                in_=x_bytes.rearrange("(p t) c -> p t c", t=4)[:, :, first : first + LOADS[i]],
            )
            x_loads.append(codes_in)

        scale = keep.tile([P, 4], F32, name="scale")
        nc.sync.dma_start(out=scale[:], in_=x_scale.rearrange("(p t) o -> p (t o)", t=4))
        load_a("ar", ar, 0)
        load_x()
        load_a("aim", aim, 0)
        load_a("ar", ar, 1)
        load_a("aim", aim, 1)
        load_x()
        load_x()
        w2_rows = keep.tile([P, 3, F], BF16, name="w2_rows", align_bytes=64)
        for m, weights in enumerate((cr, cim, phi)):
            nc.sync.dma_start(out=w2_rows[:, m, :], in_=weights)
        gain_plain = keep.tile([P, F], BF16, name="gain_plain")
        nc.sync.dma_start(out=gain_plain[:], in_=g1.partition_broadcast(P))
        while len(x_loads) < len(LOADS):
            load_x()

        quarter = keep.tile([P, 1], F32, name="quarter")
        nc.vector.memset(quarter[:], 0.25)
        warm = keep.tile([P, 1], F32, name="warm")
        nc.scalar.activation(out=warm[:], in_=quarter[:], func=ACT.Sqrt)

        x_wide, x_grouped, x_codes, x_scales = {}, {}, {}, {}

        def widen(k):
            n = CHUNKS[k]
            source, first = (x_loads[k], 0) if k < 3 else (x_loads[3 + (k - 3) // 2], (k - 3) % 2 * n)
            wide = stage.tile([P, 4, n], BF16, name="x_wide", align_bytes=64)
            for t in range(4):
                nc.vector.tensor_scalar(
                    out=wide[:, t, :],
                    in0=source[:, t, first : first + n].bitcast(FP8),
                    scalar1=scale[:, t : t + 1],
                    scalar2=None,
                    op0=ALU.mult,
                )
            x_wide[k] = wide

        def group_x(k, side):
            n = CHUNKS[k]
            if side == 0:
                grouped = stage.tile([P, n, 4], BF16, name="x_grouped", align_bytes=64)
                x_grouped[k] = grouped
            cols = slice(side * n // 2, (side + 1) * n // 2)
            nc.vector.tensor_copy(
                out=x_grouped[k][:, cols, :].rearrange("p (c i) t -> p c t i", i=4),
                in_=x_wide[k][:, :, cols].rearrange("p t (c i) -> p c t i", i=4),
            )

        def quantize_x(k):
            n = CHUNKS[k]
            codes = stage.tile([P, n], U32, name="x_codes", bufs=3, align_bytes=64)
            scales = stage.tile([P, n], U8, name="x_scales", bufs=3, align_bytes=64)
            nc.vector.quantize_mx(
                out=codes[:].bitcast(FP8X4),
                scales=scales[:],
                in_=x_grouped[k][:].rearrange("p c t -> p (c t)"),
            )
            x_codes[k], x_scales[k] = codes, scales

        def prepare_x(p, side):
            if p % 2 == 1:
                if (p + 5) // 2 < len(CHUNKS):
                    group_x((p + 5) // 2, side)
            elif side == 0:
                if (p + 4) // 2 < len(CHUNKS):
                    quantize_x((p + 4) // 2)
            elif (p + 6) // 2 < len(CHUNKS):
                widen((p + 6) // 2)

        a_grouped, a_codes, a_scales = {}, {}, {}
        for name in ("ar", "aim"):
            grouped = keep.tile([P, F, 4], BF16, name=f"{name}_grouped", align_bytes=64)
            codes = keep.tile([P, F], U32, name=f"{name}_codes", align_bytes=64)
            scales = keep.tile([P, F], U8, name=f"{name}_scales", align_bytes=64)
            a_grouped[name], a_codes[name], a_scales[name] = grouped, codes, scales

        def turn_a(name, u):
            turned = psum.tile([P, 2, 2, P], F32, name="turned_a", tag="sq", bufs=4)
            for e in range(2):
                words = a_rows[name, u][:, e, :].bitcast(F32)
                for v in range(2):
                    nc.tensor.transpose(turned[:, e, v, :], words[:, v : S // 2 : 2], ident[:])
            return turned

        def group_a(name, u, turned):
            slots = slice(256 * u, 256 * u + 256)
            nc.scalar.copy(
                out=a_grouped[name][:, slots, :].bitcast(F32).rearrange("p (q e) v -> p q e v", e=2),
                in_=turned[:].rearrange("p e v q -> p q e v"),
            )

        def quantize_a(name, u):
            slots = slice(256 * u, 256 * u + 256)
            nc.vector.quantize_mx(
                out=a_codes[name][:, slots].bitcast(FP8X4),
                scales=a_scales[name][:, slots],
                in_=a_grouped[name][:, slots, :].rearrange("p j t -> p (j t)"),
            )

        w2_grouped = keep.tile([P, 3, P, 4], BF16, name="w2_grouped", align_bytes=64)
        w2_codes = keep.tile([P, 3 * P], U32, name="w2_codes", align_bytes=64)
        w2_scales = keep.tile([P, 3 * P], U8, name="w2_scales", align_bytes=64)

        def turn_and_group_w2(first, count, tag):
            turned = psum.tile([P, 2, 2, P], F32, name="turned_w2", tag=tag, bufs=1)
            for i in range(count):
                words = w2_rows[:, first + i, :].bitcast(F32)
                for v in range(2):
                    nc.tensor.transpose(turned[:, i, v, :], words[:, v : F // 2 : 2], ident[:])
            nc.vector.tensor_copy(
                out=w2_grouped[:, first : first + count, :, :].bitcast(F32),
                in_=turned[:, 0:count, :, :].rearrange("p m v g -> p m g v"),
            )

        def quantize_w2(first, count):
            cols = slice(first * P, (first + count) * P)
            nc.vector.quantize_mx(
                out=w2_codes[:, cols].bitcast(FP8X4),
                scales=w2_scales[:, cols],
                in_=w2_grouped[:, first : first + count, :, :].rearrange("p m g t -> p (m g t)"),
            )

        gain = keep.tile([P, F], F32, name="gain")

        def order_gain():
            nc.gpsimd.tensor_copy(
                out=gain[:].rearrange("p (u q e) -> p u q e", u=2, e=2),
                in_=gain_plain[:].rearrange("p (q u e) -> p u q e", u=2, e=2),
            )

        ri1, squares, sums, u1s, totals, means = {}, {}, {}, {}, {}, {}

        def first_bank(p, tile):
            k, first = (p, 0) if p < 2 else (p // 2 + 1, p % 2 * BATCH)
            cols = slice(first, first + BATCH)
            slots = slice(tile * P, tile * P + P)
            bank = psum.tile([P, 2, BATCH], F32, name="ri1", tag="sq", bufs=4)
            for i, name in enumerate(("ar", "aim")):
                nc.tensor.matmul_mx(
                    out=bank[:, i, :],
                    lhsT=a_codes[name][:, slots].bitcast(FP8X4),
                    lhsT_scale=a_scales[name][:, slots],
                    rhs=x_codes[k][:, cols].bitcast(FP8X4),
                    rhs_scale=x_scales[k][:, cols],
                    start=True,
                    stop=True,
                )
            ri1[p, tile] = bank

        def square1(p, tile):
            square = stage.tile([P, 2, BATCH], F32, name="square1", bufs=12)
            nc.scalar.activation(out=square[:], in_=ri1[p, tile][:], func=ACT.Square)
            squares[p, tile] = square

        def add_squares1(p, half, tile):
            if tile == 0:
                bank = psum.tile([P, F], F32, name="sum1", tag="c", bufs=2)
                sums[p, half] = bank
            for i in range(2):
                nc.tensor.matmul(
                    out=sums[p, half][:, tile * P : tile * P + P],
                    lhsT=squares[p, tile][:, i, half * P : half * P + P],
                    rhs=ident[:],
                    is_transpose=True,
                    start=(i == 0),
                    stop=(i == 1),
                )

        def root1(p, half):
            if half == 0:
                total = stage.tile([P, 2], F32, name="total", bufs=6)
                totals[p] = total
            u1 = stage.tile([P, F], F32, name="u1", bufs=8)
            nc.scalar.activation(
                out=u1[:],
                in_=sums[p, half][:],
                func=ACT.Sqrt,
                bias=quarter[:, 0:1],
                accum_out=totals[p][:, half : half + 1],
            )
            u1s[p, half] = u1

        def average(p):
            mean = stage.tile([P, 2], F32, name="mean", bufs=6)
            nc.vector.tensor_scalar(
                out=mean[:], in0=totals[p][:], scalar1=1.0 / F, scalar2=None, op0=ALU.mult
            )
            means[p] = mean

        n1s, n1_turned, n1_grouped, n1_codes, n1_scales = {}, {}, {}, {}, {}

        def centre(p, half):
            n1 = stage.tile([P, F], BF16, name="n1", bufs=6, align_bytes=64)
            nc.vector.scalar_tensor_tensor(
                out=n1[:],
                in0=u1s[p, half][:],
                scalar=means[p][:, half : half + 1],
                in1=gain[:],
                op0=ALU.subtract,
                op1=ALU.mult,
            )
            n1s[p, half] = n1

        def turn_n1(p, half):
            if half == 0:
                bank = psum.tile([P, 2, 2, P], F32, name="n1_turned", tag="tr", bufs=1)
                n1_turned[p] = bank
            words = n1s[p, half][:].bitcast(F32)
            for u in range(2):
                nc.tensor.transpose(n1_turned[p][:, half, u, :], words[:, u * P : u * P + P], ident[:])

        def group_n1(p):
            grouped = stage.tile([P, BATCH, 4], BF16, name="n1_grouped", bufs=3, align_bytes=64)
            nc.vector.tensor_copy(
                out=grouped[:].bitcast(F32).rearrange("p (h r) u -> p h r u", h=2),
                in_=n1_turned[p][:].rearrange("p h u r -> p h r u"),
            )
            n1_grouped[p] = grouped

        def quantize_n1(p):
            codes = stage.tile([P, BATCH], U32, name="n1_codes", bufs=4, align_bytes=64)
            scales = stage.tile([P, BATCH], U8, name="n1_scales", bufs=4, align_bytes=64)
            nc.vector.quantize_mx(
                out=codes[:].bitcast(FP8X4),
                scales=scales[:],
                in_=n1_grouped[p][:].rearrange("p c t -> p (c t)"),
            )
            n1_codes[p], n1_scales[p] = codes, scales

        ri2, outs, squares2 = {}, {}, {}

        def second_bank(p):
            late = p >= N_BATCHES - LATE
            bank = psum.tile([P, 2, 2 * G], F32, name="ri2", tag="sq" if late else "tr", bufs=4 if late else 1)
            for half in range(2):
                cols = slice(half * P, half * P + P)
                nc.tensor.matmul_mx(
                    out=bank[:, half, :],
                    lhsT=n1_codes[p][:, cols].bitcast(FP8X4),
                    lhsT_scale=n1_scales[p][:, cols],
                    rhs=w2_codes[:, 0 : 2 * G].bitcast(FP8X4),
                    rhs_scale=w2_scales[:, 0 : 2 * G],
                    start=True,
                    stop=True,
                )
            ri2[p] = bank

        def first_order(p):
            late = p >= N_BATCHES - LATE
            bank = psum.tile([P, 2, BATCH], F32, name="out", tag="sq" if late else "o", bufs=4 if late else 1)
            nc.tensor.matmul_mx(
                out=bank[:, 0, :],
                lhsT=w2_codes[:, 2 * G : 3 * G].bitcast(FP8X4),
                lhsT_scale=w2_scales[:, 2 * G : 3 * G],
                rhs=n1_codes[p][:].bitcast(FP8X4),
                rhs_scale=n1_scales[p][:],
                start=True,
                stop=True,
            )
            outs[p] = bank

        def store_s1(p):
            s1 = stage.tile([P, BATCH], F32, name="s1", bufs=3)
            nc.vector.tensor_copy(out=s1[:], in_=outs[p][:, 0, :])
            nc.sync.dma_start(out=out_0[:, p * BATCH : p * BATCH + BATCH], in_=s1[:])

        def square2(p):
            square = stage.tile([P, 2, 2 * G], F32, name="square2", bufs=3)
            nc.scalar.activation(out=square[:], in_=ri2[p][:], func=ACT.Square)
            squares2[p] = square

        def add_squares2(p):
            for half in range(2):
                for i in range(2):
                    nc.tensor.matmul(
                        out=outs[p][:, 1, half * P : half * P + P],
                        lhsT=squares2[p][:, half, i * G : i * G + G],
                        rhs=ident[:],
                        is_transpose=True,
                        start=(i == 0),
                        stop=(i == 1),
                    )

        def late_add_squares2(p):
            if p >= N_BATCHES - LATE:
                add_squares2(p)

        def store_u2(p):
            u2 = stage.tile([P, BATCH], F32, name="u2", bufs=3)
            nc.scalar.activation(out=u2[:], in_=outs[p][:, 1, :], func=ACT.Sqrt, bias=quarter[:, 0:1])
            nc.sync.dma_start(out=out_1[:, p * BATCH : p * BATCH + BATCH], in_=u2[:])

        turned = turn_a("ar", 0)
        group_a("ar", 0, turned)
        widen(0)
        group_x(0, 0)
        group_x(0, 1)
        quantize_a("ar", 0)
        quantize_x(0)
        turned = turn_a("aim", 0)
        group_a("aim", 0, turned)
        quantize_a("aim", 0)
        widen(1)
        turned = turn_a("ar", 1)
        group_a("ar", 1, turned)
        quantize_a("ar", 1)
        turned = turn_a("aim", 1)
        group_a("aim", 1, turned)
        group_x(1, 0)
        quantize_a("aim", 1)
        group_x(1, 1)
        quantize_x(1)
        order_gain()
        widen(2)
        group_x(2, 0)
        group_x(2, 1)
        first_bank(0, 0)
        first_bank(0, 1)

        loop_order = [
            (lambda p: add_squares1(p, 1, 3), 1),
            (lambda p: square1(p, 0), 0),
            (group_n1, 3),
            (lambda p: first_bank(p, 2), 0),
            (second_bank, 4),
            (lambda p: first_bank(p, 3), 0),
            (lambda p: square1(p, 1), 0),
            (lambda p: centre(p, 0), 2),
            (lambda p: centre(p, 1), 2),
            (store_u2, 5),
            (lambda p: root1(p, 0), 1),
            (lambda p: square1(p, 2), 0),
            (square2, 4),
            (lambda p: root1(p, 1), 1),
            (first_order, 4),
            (lambda p: first_bank(p, 0), -1),
            (quantize_n1, 3),
            (lambda p: first_bank(p, 1), -1),
            (lambda p: prepare_x(p, 0), 0),
            (lambda p: add_squares1(p, 0, 0), 0),
            (store_s1, 4),
            (lambda p: add_squares1(p, 0, 1), 0),
            (lambda p: square1(p, 3), 0),
            (lambda p: add_squares1(p, 0, 2), 0),
            (lambda p: turn_n1(p, 0), 2),
            (lambda p: turn_n1(p, 1), 2),
            (add_squares2, 4),
            (lambda p: add_squares1(p, 1, 0), 0),
            (lambda p: add_squares1(p, 1, 1), 0),
            (lambda p: add_squares1(p, 1, 2), 0),
            (lambda p: add_squares1(p, 0, 3), 0),
            (lambda p: prepare_x(p, 1), 0),
            (average, 1),
        ]
        drain_order = [
            (lambda p: add_squares1(p, 1, 3), 1),
            (second_bank, 4),
            (first_order, 4),
            (group_n1, 3),
            (lambda p: root1(p, 0), 1),
            (lambda p: centre(p, 0), 2),
            (lambda p: centre(p, 1), 2),
            (lambda p: root1(p, 1), 1),
            (square2, 4),
            (late_add_squares2, 5),
            (lambda p: turn_n1(p, 0), 2),
            (store_u2, 5),
            (lambda p: turn_n1(p, 1), 2),
            (quantize_n1, 3),
            (store_s1, 4),
            (average, 1),
        ]
        for p in range(N_BATCHES + 5):
            if p == 1:
                turn_and_group_w2(0, 2, "tr")
                turn_and_group_w2(2, 1, "o")
            if p == 2:
                quantize_w2(0, 2)
                quantize_w2(2, 1)
            for stage_of, behind in loop_order if p < N_BATCHES else drain_order:
                if 0 <= p - behind < N_BATCHES:
                    stage_of(p - behind)
